import numpy as np
import ml_dtypes


def mxq(x, axis, fmt="e4m3"):
    dtype, down = {"e4m3": (ml_dtypes.float8_e4m3fn, 7), "e5m2": (ml_dtypes.float8_e5m2, 14)}[fmt]
    v = np.moveaxis(np.asarray(x, np.float32).astype(ml_dtypes.bfloat16).astype(np.float64), axis, -1)
    blocks = v.reshape(v.shape[:-1] + (-1, 32))
    amax = np.abs(blocks).max(-1, keepdims=True)
    byte = np.maximum(np.where(amax > 0, np.frexp(amax)[1] - 1 + 127, 0) - down, 1)
    scale = np.exp2(byte - 127.0)
    codes = (blocks / scale).astype(np.float32).astype(dtype).astype(np.float64)
    return np.moveaxis((codes * scale).reshape(v.shape), -1, axis)


WIDE = False


def mx_kscale(k):
    if not WIDE:
        return np.ones(k)
    levels = np.array([10, -10, 5, -5, 0])
    if k % 512:
        return np.exp2(np.random.permutation(np.resize(levels, k // 32))).repeat(32)
    a = np.empty((k // 512, 16))
    for p in range(k // 512):
        a[p, :8] = np.random.permutation(np.resize(levels, 8))
        for g in range(8):
            far = levels[np.abs(levels - a[p, g]) >= 10]
            a[p, g + 8] = far[np.random.randint(len(far))]
    return np.exp2(a.ravel()).repeat(32)


def f64(x):
    return np.asarray(x).astype(np.float64)


def striped(idx):
    return np.tile(idx.reshape(-1, 16).T, (8, 1)).astype(np.uint16)


def unstriped(offs):
    return offs[:16].T.reshape(-1).astype(np.int64)


def striped8(idx):
    return np.concatenate([x.reshape(-1, 16).T for x in idx]).astype(np.uint16)


def runs(offs, k):
    lists = np.stack([offs[16 * r : 16 * r + 16].T.reshape(-1) for r in range(8)]).astype(np.int64)
    return lists[np.arange(k) % 512 // 64]


def pack_weight(w):
    k, n = w.shape
    w = f64(np.asarray(w, np.float32).astype(ml_dtypes.bfloat16)).reshape(k // 32, 32, n)
    amax = np.abs(w).max(1)
    byte = np.clip(np.where(amax > 0, np.frexp(amax)[1] - 1 + 127 - 7, 1), 1, 254)
    scaled = (w * np.exp2(127.0 - byte)[:, None, :]).reshape(k, n).astype(np.float32)
    words = np.ascontiguousarray(scaled.reshape(k // 512, 128, 4, n).transpose(0, 1, 3, 2)).astype(ml_dtypes.float8_e4m3fn).view(np.uint8)
    return words, np.ascontiguousarray(byte.astype(np.uint8).reshape(k // 512, 16, n))


def unpack_weight(words, scales):
    g, p, n, _ = words.shape
    vals = np.ascontiguousarray(words).view(ml_dtypes.float8_e4m3fn).astype(np.float64) * np.repeat(np.exp2(scales.astype(np.float64) - 127.0), 8, axis=1)[..., None]
    return vals.transpose(0, 1, 3, 2).reshape(g * 512, n)


K, T, S, N, G, H = 512, 2048, 256, 512, 2048, 512


def setup_inputs():
    n = np.random.standard_normal
    s = mx_kscale(K)[:, None]
    u = mx_kscale(K)
    packed_xT = pack_weight(n((K, T)) * s)
    packed_dT = pack_weight(n((K, G)) / s)
    packed_w1 = pack_weight(n((H, N)) / np.sqrt(2 * H) / u[:, None])
    packed_w2 = pack_weight(n((K, N)) / np.sqrt(2 * K) / s)
    return {
        "x_words": packed_xT[0],
        "x_scales": packed_xT[1],
        "d_words": packed_dT[0],
        "d_scales": packed_dT[1],
        "gn": (np.random.uniform(0.5, 1.5, (H, 1)) * u[:, None]).astype(np.float32),
        "w1_words": packed_w1[0],
        "w1_scales": packed_w1[1],
        "w2_words": packed_w2[0],
        "w2_scales": packed_w2[1],
        "offs": striped(np.random.permutation(T)[:S]),
        "k1": striped8(np.random.randint(0, G, (8, H))),
        "two": striped(np.random.permutation(T)[:S]),
        "n1": striped(np.random.permutation(S)),
        "n2": striped(np.random.permutation(S)),
    }


def reference(x_words, x_scales, d_words, d_scales, gn, w1_words, w1_scales, w2_words, w2_scales, offs, k1, two, n1, n2):
    d_k1 = unpack_weight(d_words, d_scales)[np.arange(K)[:, None], runs(k1, K)]
    xq = unpack_weight(x_words, x_scales)[:, unstriped(offs)]
    s = 0.0625 * (d_k1.T @ xq)
    z = f64(gn) * s
    x_two = unpack_weight(x_words, x_scales)[:, unstriped(two)]
    h = unpack_weight(w1_words, w1_scales).T @ mxq(z, 0, "e4m3") + unpack_weight(w2_words, w2_scales).T @ x_two
    ds = np.zeros((N, S))
    ds[:, unstriped(n1)] = h
    return np.maximum(h, ds[:, unstriped(n2)])

@@ -1,0 +1,171 @@
+from contextlib import ExitStack
+
+import concourse.mybir as mybir
+
+K, T, S, N, G, H = 512, 2048, 256, 512, 2048, 512
+FLOPS = 2 * S * (K * H + H * N + K * N)
+
+F32 = mybir.dt.float32
+BF16 = mybir.dt.bfloat16
+I32 = mybir.dt.int32
+U32 = mybir.dt.uint32
+U16 = mybir.dt.uint16
+U8 = mybir.dt.uint8
+FP8X4 = mybir.dt.float8_e4m3fn_x4
+COPY = mybir.ActivationFunctionType.Copy
+MULT = mybir.AluOpType.mult
+MAX = mybir.AluOpType.max
+
+P = 128
+PACK = 4
+QUAD = 32
+GROUP = 16
+HALF = S // 2
+HALF_COLS = HALF // GROUP
+TILES = N // P
+
+
+def tile_picked_kmixirelay_none_p_kernel(
+    tc, x_words, x_scales, d_words, d_scales, gn, w1_words, w1_scales, w2_words, w2_scales, offs, k1, two, n1, n2, out
+):
+    nc = tc.nc
+
+    def words_of(dram):
+        return dram[0].rearrange("p n t -> p (n t)").bitcast(I32)
+
+    with ExitStack() as ctx:
+        keep = ctx.enter_context(tc.tile_pool(name="keep", bufs=1))
+        psum = ctx.enter_context(tc.psum_pool(name="psum", bufs=1))
+
+        def sb(name, shape, dtype, tag=None):
+            return keep.tile(shape, dtype, name=name, tag=tag or name, align_bytes=64)
+
+        k1_l = sb("k1_l", [P, H // GROUP], U16)
+        offs_l = sb("offs_l", [P, S // GROUP], U16)
+        two_l = sb("two_l", [P, S // GROUP], U16)
+        n1_l = sb("n1_l", [P, S // GROUP], U16)
+        n2_l = sb("n2_l", [P, S // GROUP], U16)
+        d_tab = sb("d_tab", [P, G], U32)
+        x_tab = sb("x_tab", [P, T], U32)
+        ds_tab = sb("ds_tab", [P, G], U8, "ds_then_w")
+        xs_tab = sb("xs_tab", [P, T], U8, "xs_then_w1_s")
+        w2_s = sb("w2_s", [P, N], U8)
+        gn_t = sb("gn_t", [P, PACK], F32)
+        gain = sb("gain", [P, PACK], F32)
+
+        nc.vector.memset(ds_tab[:].bitcast(I32), 0)
+        nc.vector.memset(xs_tab[:].bitcast(I32), 0)
+        nc.vector.memset(w2_s[:].bitcast(I32), 0)
+
+        def load_scale_rows(queues, tile, dram):
+            rows = dram[0].bitcast(I32)
+            for j in range(PACK):
+                queues[j].dma_start(tile[j:P:QUAD, :].bitcast(I32), rows[j:16:PACK, :])
+
+        for tile, dram in ((k1_l, k1), (offs_l, offs), (two_l, two), (n1_l, n1), (n2_l, n2)):
+            nc.sync.dma_start(tile[:], dram)
+        nc.sync.dma_start(d_tab[:].bitcast(I32), words_of(d_words))
+        nc.sync.dma_start(x_tab[:].bitcast(I32), words_of(x_words))
+        nc.scalar.dma_start(ds_tab[0:P:8, :].bitcast(I32), d_scales[0].bitcast(I32))
+        load_scale_rows([nc.scalar] * PACK, xs_tab, x_scales)
+        nc.gpsimd.dma_start(gn_t[:], gn.rearrange("(p t) o -> p (t o)", t=PACK))
+        load_scale_rows([nc.scalar] + [nc.gpsimd] * 3, w2_s, w2_scales)
+
+        nc.scalar.activation(gain[:], gn_t[:], COPY, scale=0.0625)
+
+        ds_g = sb("ds_g", [P, H], U8, "picked")
+        nc.vector.tensor_copy(ds_g[:], ds_tab[:].indirect(k1_l[:]))
+        w_t = sb("w_t", [P, 2 * N], U32, "ds_then_w")
+        w2_t = w_t[:, 0:N]
+        w1_t = w_t[:, N : 2 * N]
+        nc.sync.dma_start(w2_t.bitcast(I32), words_of(w2_words))
+        nc.sync.dma_start(w1_t.bitcast(I32), words_of(w1_words))
+        key_s = sb("key_s", [P, H], U8)
+        nc.vector.tensor_copy(
+            key_s[:].rearrange("p (t mm i) -> p mm t i", t=PACK, i=16),
+            ds_g[:].rearrange("p (mm i t) -> p mm t i", t=PACK, i=16),
+        )
+        for j in range(1, PACK):
+            nc.scalar.dma_start(key_s[j:P:QUAD, :].bitcast(I32), key_s[8 * j : P : QUAD, :].bitcast(I32))
+
+        xq_s = sb("xq_s", [P, S], U8)
+        nc.vector.tensor_copy(xq_s[:], xs_tab[:].indirect(offs_l[:]))
+
+        d_g = sb("d_g", [P, H], U32, "picked")
+        two_s = sb("two_s", [P, S], U8)
+        nc.vector.tensor_copy(d_g[:], d_tab[:].indirect(k1_l[:]))
+        nc.vector.tensor_copy(two_s[:], xs_tab[:].indirect(two_l[:]))
+        w1_s = sb("w1_s", [P, N], U8, "xs_then_w1_s")
+        nc.gpsimd.memset(w1_s[:].bitcast(I32), 0)
+        load_scale_rows([nc.scalar] * 3 + [nc.gpsimd], w1_s, w1_scales)
+        key_w = sb("key_w", [P, H], U32)
+        nc.vector.tensor_copy(
+            key_w[:].rearrange("p (t mm i) -> p mm t i", t=PACK, i=4),
+            d_g[:].rearrange("p (mm i t) -> p mm t i", t=PACK, i=4),
+        )
+
+        h_bank = [psum.tile([P, S], F32, name="h_bank%d" % t) for t in range(TILES)]
+        h_sb = [[sb("h_sb%d_%d" % (t, u), [P, HALF], F32) for u in range(2)] for t in range(TILES)]
+        ds = [sb("ds%d" % t, [P, S], F32) for t in range(TILES)]
+
+        xq_w = sb("xq_w", [P, S], U32, "picked")
+        s_bank = [psum.tile([P, PACK, HALF], F32, name="s_bank%d" % u) for u in range(2)]
+        for u in range(2):
+            cols = slice(u * HALF, (u + 1) * HALF)
+            nc.vector.tensor_copy(xq_w[:, cols], x_tab[:].indirect(offs_l[:, u * HALF_COLS : (u + 1) * HALF_COLS]))
+            for t in range(PACK):
+                kc = slice(t * P, (t + 1) * P)
+                nc.tensor.matmul_mx(
+                    out=s_bank[u][:, t, :], lhsT=key_w[:, kc].bitcast(FP8X4), lhsT_scale=key_s[:, kc],
+                    rhs=xq_w[:, cols].bitcast(FP8X4), rhs_scale=xq_s[:, cols], start=True, stop=True,
+                )
+
+        for u in range(2):
+            cols = slice(u * HALF, (u + 1) * HALF)
+            lcols = slice(u * HALF_COLS, (u + 1) * HALF_COLS)
+            z_bf = sb("z_bf%d" % u, [P, HALF, PACK], BF16, "z_bf")
+            nc.vector.tensor_tensor(
+                z_bf[:], s_bank[u][:].rearrange("p t n -> p n t"), gain[:].unsqueeze(1).broadcast_to([P, HALF, PACK]), MULT
+            )
+            two_w = sb("two_w%d" % u, [P, HALF], U32, "picked")
+            nc.vector.tensor_copy(two_w[:], x_tab[:].indirect(two_l[:, lcols]))
+            for t in range(TILES):
+                mc = slice(t * P, (t + 1) * P)
+                nc.tensor.matmul_mx(
+                    out=h_bank[t][:, cols], lhsT=w2_t[:, mc].bitcast(FP8X4), lhsT_scale=w2_s[:, mc],
+                    rhs=two_w[:].bitcast(FP8X4), rhs_scale=two_s[:, cols], start=True, stop=False,
+                )
+            z_w = sb("z_w%d" % u, [P, HALF], U32)
+            z_s = sb("z_s%d" % u, [P, HALF], U8)
+            nc.vector.quantize_mx(out=z_w[:].bitcast(FP8X4), scales=z_s[:], in_=z_bf[:].rearrange("p n t -> p (n t)"))
+            for t in range(TILES):
+                mc = slice(t * P, (t + 1) * P)
+                nc.tensor.matmul_mx(
+                    out=h_bank[t][:, cols], lhsT=w1_t[:, mc].bitcast(FP8X4), lhsT_scale=w1_s[:, mc],
+                    rhs=z_w[:].bitcast(FP8X4), rhs_scale=z_s[:], start=False, stop=True,
+                )
+                if u == 0 and t == 0:
+                    nc.scalar.copy(h_sb[t][u][:], h_bank[t][:, cols])
+                else:
+                    nc.vector.tensor_copy(h_sb[t][u][:], h_bank[t][:, cols])
+            if u == 0:
+                for t in range(TILES):
+                    nc.scalar.activation(ds[t][:].indirect(n1_l[:, lcols]), h_sb[t][u][:], COPY)
+
+        def scatter_second(t):
+            nc.scalar.activation(ds[t][:].indirect(n1_l[:, HALF_COLS:]), h_sb[t][1][:], COPY)
+
+        def fetch(t):
+            res = sb("res%d" % t, [P, S], F32)
+            for u in range(2):
+                cols = slice(u * HALF, (u + 1) * HALF)
+                got = sb("got%d_%d" % (t, u), [P, HALF], F32)
+                nc.scalar.activation(got[:], ds[t][:].indirect(n2_l[:, u * HALF_COLS : (u + 1) * HALF_COLS]), COPY)
+                nc.vector.tensor_tensor(res[:, cols], h_sb[t][u][:], got[:], MAX)
+            nc.sync.dma_start(out[t * P : (t + 1) * P, :], res[:])
+
+        scatter_second(0)
+        for t in range(TILES):
+            if t + 1 < TILES:
+                scatter_second(t + 1)
+            fetch(t)

@@ -35,6 +35,7 @@ def tile_picked_kmixirelay_none_p_kernel(
 
     with ExitStack() as ctx:
         keep = ctx.enter_context(tc.tile_pool(name="keep", bufs=1))
+        reuse = ctx.enter_context(tc.tile_pool(name="reuse", bufs=1))
         psum = ctx.enter_context(tc.psum_pool(name="psum", bufs=1))
 
         def sb(name, shape, dtype, tag=None):
@@ -46,58 +47,55 @@ def tile_picked_kmixirelay_none_p_kernel(
         n1_l = sb("n1_l", [P, S // GROUP], U16)
         n2_l = sb("n2_l", [P, S // GROUP], U16)
         d_tab = sb("d_tab", [P, G], U32)
-        x_tab = sb("x_tab", [P, T], U32)
-        ds_tab = sb("ds_tab", [P, G], U8, "ds_then_w")
-        xs_tab = sb("xs_tab", [P, T], U8, "xs_then_w1_s")
+        ds_tab = sb("ds_tab", [P, G], U8)
+        xs_tab = sb("xs_tab", [P, T], U8)
         w2_s = sb("w2_s", [P, N], U8)
-        gn_t = sb("gn_t", [P, PACK], F32)
+        gn_t = sb("gn_t", [P, PACK], F32, "gn_then_x")
         gain = sb("gain", [P, PACK], F32)
-
-        nc.vector.memset(ds_tab[:].bitcast(I32), 0)
-        nc.vector.memset(xs_tab[:].bitcast(I32), 0)
-        nc.vector.memset(w2_s[:].bitcast(I32), 0)
 
         def load_scale_rows(queues, tile, dram):
             rows = dram[0].bitcast(I32)
             for j in range(PACK):
                 queues[j].dma_start(tile[j:P:QUAD, :].bitcast(I32), rows[j:16:PACK, :])
 
+        nc.gpsimd.memset(ds_tab[:].bitcast(I32), 0)
+        nc.vector.memset(xs_tab[:].bitcast(I32), 0)
+        nc.scalar.dma_start(gn_t[:], gn.rearrange("(p t) o -> p (t o)", t=PACK))
         for tile, dram in ((k1_l, k1), (offs_l, offs), (two_l, two), (n1_l, n1), (n2_l, n2)):
             nc.sync.dma_start(tile[:], dram)
-        nc.sync.dma_start(d_tab[:].bitcast(I32), words_of(d_words))
-        nc.sync.dma_start(x_tab[:].bitcast(I32), words_of(x_words))
         nc.scalar.dma_start(ds_tab[0:P:8, :].bitcast(I32), d_scales[0].bitcast(I32))
-        load_scale_rows([nc.scalar] * PACK, xs_tab, x_scales)
-        nc.gpsimd.dma_start(gn_t[:], gn.rearrange("(p t) o -> p (t o)", t=PACK))
-        load_scale_rows([nc.scalar] + [nc.gpsimd] * 3, w2_s, w2_scales)
+        nc.sync.dma_start(d_tab[:].bitcast(I32), words_of(d_words))
+        load_scale_rows([nc.sync] * PACK, xs_tab, x_scales)
+        load_scale_rows([nc.gpsimd] * PACK, w2_s, w2_scales)
 
         nc.scalar.activation(gain[:], gn_t[:], COPY, scale=0.0625)
+        x_tab = sb("x_tab", [P, T], U32, "gn_then_x")
+        nc.sync.dma_start(x_tab[:].bitcast(I32), words_of(x_words))
 
-        ds_g = sb("ds_g", [P, H], U8, "picked")
+        ds_g = reuse.tile([P, H], U8, name="ds_g", align_bytes=64, offset=8 * N - H // 2)
         nc.vector.tensor_copy(ds_g[:], ds_tab[:].indirect(k1_l[:]))
-        w_t = sb("w_t", [P, 2 * N], U32, "ds_then_w")
-        w2_t = w_t[:, 0:N]
-        w1_t = w_t[:, N : 2 * N]
-        nc.sync.dma_start(w2_t.bitcast(I32), words_of(w2_words))
-        nc.sync.dma_start(w1_t.bitcast(I32), words_of(w1_words))
         key_s = sb("key_s", [P, H], U8)
         nc.vector.tensor_copy(
             key_s[:].rearrange("p (t mm i) -> p mm t i", t=PACK, i=16),
             ds_g[:].rearrange("p (mm i t) -> p mm t i", t=PACK, i=16),
         )
         for j in range(1, PACK):
-            nc.scalar.dma_start(key_s[j:P:QUAD, :].bitcast(I32), key_s[8 * j : P : QUAD, :].bitcast(I32))
+            nc.sync.dma_start(key_s[j:P:QUAD, :].bitcast(I32), key_s[8 * j : P : QUAD, :].bitcast(I32))
+        w_t = reuse.tile([P, 2 * N], U32, name="w_t", align_bytes=64, offset=0)
+        w1_s = reuse.tile([P, N], U8, name="w1_s", align_bytes=64, offset=8 * N)
+        w2_t = w_t[:, 0:N]
+        w1_t = w_t[:, N : 2 * N]
+        nc.sync.dma_start(w2_t.bitcast(I32), words_of(w2_words))
+        nc.sync.dma_start(w1_t.bitcast(I32), words_of(w1_words))
+        load_scale_rows([nc.sync] * PACK, w1_s, w1_scales)
 
         xq_s = sb("xq_s", [P, S], U8)
         nc.vector.tensor_copy(xq_s[:], xs_tab[:].indirect(offs_l[:]))
 
-        d_g = sb("d_g", [P, H], U32, "picked")
+        d_g = sb("d_g", [P, H], U32)
         two_s = sb("two_s", [P, S], U8)
         nc.vector.tensor_copy(d_g[:], d_tab[:].indirect(k1_l[:]))
         nc.vector.tensor_copy(two_s[:], xs_tab[:].indirect(two_l[:]))
-        w1_s = sb("w1_s", [P, N], U8, "xs_then_w1_s")
-        nc.gpsimd.memset(w1_s[:].bitcast(I32), 0)
-        load_scale_rows([nc.scalar] * 3 + [nc.gpsimd], w1_s, w1_scales)
         key_w = sb("key_w", [P, H], U32)
         nc.vector.tensor_copy(
             key_w[:].rearrange("p (t mm i) -> p mm t i", t=PACK, i=4),
@@ -108,9 +106,10 @@ def tile_picked_kmixirelay_none_p_kernel(
         h_sb = [[sb("h_sb%d_%d" % (t, u), [P, HALF], F32) for u in range(2)] for t in range(TILES)]
         ds = [sb("ds%d" % t, [P, S], F32) for t in range(TILES)]
 
-        xq_w = sb("xq_w", [P, S], U32, "picked")
+        xq_w = sb("xq_w", [P, S], U32)
         s_bank = [psum.tile([P, PACK, HALF], F32, name="s_bank%d" % u) for u in range(2)]
-        for u in range(2):
+
+        def score(u):
             cols = slice(u * HALF, (u + 1) * HALF)
             nc.vector.tensor_copy(xq_w[:, cols], x_tab[:].indirect(offs_l[:, u * HALF_COLS : (u + 1) * HALF_COLS]))
             for t in range(PACK):
@@ -120,6 +119,20 @@ def tile_picked_kmixirelay_none_p_kernel(
                     rhs=xq_w[:, cols].bitcast(FP8X4), rhs_scale=xq_s[:, cols], start=True, stop=True,
                 )
 
+        def project(u):
+            cols = slice(u * HALF, (u + 1) * HALF)
+            two_w = sb("two_w%d" % u, [P, HALF], U32, "two_w")
+            nc.vector.tensor_copy(two_w[:], x_tab[:].indirect(two_l[:, u * HALF_COLS : (u + 1) * HALF_COLS]))
+            for t in range(TILES):
+                mc = slice(t * P, (t + 1) * P)
+                nc.tensor.matmul_mx(
+                    out=h_bank[t][:, cols], lhsT=w2_t[:, mc].bitcast(FP8X4), lhsT_scale=w2_s[:, mc],
+                    rhs=two_w[:].bitcast(FP8X4), rhs_scale=two_s[:, cols], start=True, stop=False,
+                )
+
+        score(0)
+        project(0)
+        score(1)
         for u in range(2):
             cols = slice(u * HALF, (u + 1) * HALF)
             lcols = slice(u * HALF_COLS, (u + 1) * HALF_COLS)
@@ -127,14 +140,8 @@ def tile_picked_kmixirelay_none_p_kernel(
             nc.vector.tensor_tensor(
                 z_bf[:], s_bank[u][:].rearrange("p t n -> p n t"), gain[:].unsqueeze(1).broadcast_to([P, HALF, PACK]), MULT
             )
-            two_w = sb("two_w%d" % u, [P, HALF], U32, "picked")
-            nc.vector.tensor_copy(two_w[:], x_tab[:].indirect(two_l[:, lcols]))
-            for t in range(TILES):
-                mc = slice(t * P, (t + 1) * P)
-                nc.tensor.matmul_mx(
-                    out=h_bank[t][:, cols], lhsT=w2_t[:, mc].bitcast(FP8X4), lhsT_scale=w2_s[:, mc],
-                    rhs=two_w[:].bitcast(FP8X4), rhs_scale=two_s[:, cols], start=True, stop=False,
-                )
+            if u == 1:
+                project(1)
             z_w = sb("z_w%d" % u, [P, HALF], U32)
             z_s = sb("z_s%d" % u, [P, HALF], U8)
             nc.vector.quantize_mx(out=z_w[:].bitcast(FP8X4), scales=z_s[:], in_=z_bf[:].rearrange("p n t -> p (n t)"))

@@ -36,6 +36,7 @@ def tile_picked_kmixirelay_none_p_kernel(
     with ExitStack() as ctx:
         keep = ctx.enter_context(tc.tile_pool(name="keep", bufs=1))
         reuse = ctx.enter_context(tc.tile_pool(name="reuse", bufs=1))
+        reuse2 = ctx.enter_context(tc.tile_pool(name="reuse2", bufs=1))
         psum = ctx.enter_context(tc.psum_pool(name="psum", bufs=1))
 
         def sb(name, shape, dtype, tag=None):
@@ -46,33 +47,34 @@ def tile_picked_kmixirelay_none_p_kernel(
         two_l = sb("two_l", [P, S // GROUP], U16)
         n1_l = sb("n1_l", [P, S // GROUP], U16)
         n2_l = sb("n2_l", [P, S // GROUP], U16)
-        d_tab = sb("d_tab", [P, G], U32)
+        d_tab = sb("d_tab", [P, G], U32, "d_tab_then_w")
+        x_tab = sb("x_tab", [P, T], U32)
         ds_tab = sb("ds_tab", [P, G], U8)
-        xs_tab = sb("xs_tab", [P, T], U8)
+        xs_tab = reuse.tile([P, T], U8, name="xs_tab", align_bytes=64, offset=0)
         w2_s = sb("w2_s", [P, N], U8)
-        gn_t = sb("gn_t", [P, PACK], F32, "gn_then_x")
+        gn_t = sb("gn_t", [P, PACK], F32)
         gain = sb("gain", [P, PACK], F32)
 
-        def load_scale_rows(queues, tile, dram):
+        def load_scale_rows(queue, tile, dram):
             rows = dram[0].bitcast(I32)
             for j in range(PACK):
-                queues[j].dma_start(tile[j:P:QUAD, :].bitcast(I32), rows[j:16:PACK, :])
+                queue.dma_start(tile[j:P:QUAD, :].bitcast(I32), rows[j:16:PACK, :])
 
-        nc.gpsimd.memset(ds_tab[:].bitcast(I32), 0)
+        nc.vector.memset(ds_tab[:, 0 : G // 2].bitcast(I32), 0)
+        nc.gpsimd.memset(ds_tab[:, G // 2 : G].bitcast(I32), 0)
         nc.vector.memset(xs_tab[:].bitcast(I32), 0)
         nc.scalar.dma_start(gn_t[:], gn.rearrange("(p t) o -> p (t o)", t=PACK))
         for tile, dram in ((k1_l, k1), (offs_l, offs), (two_l, two), (n1_l, n1), (n2_l, n2)):
             nc.sync.dma_start(tile[:], dram)
         nc.scalar.dma_start(ds_tab[0:P:8, :].bitcast(I32), d_scales[0].bitcast(I32))
         nc.sync.dma_start(d_tab[:].bitcast(I32), words_of(d_words))
-        load_scale_rows([nc.sync] * PACK, xs_tab, x_scales)
-        load_scale_rows([nc.gpsimd] * PACK, w2_s, w2_scales)
+        nc.sync.dma_start(x_tab[:].bitcast(I32), words_of(x_words))
+        load_scale_rows(nc.scalar, xs_tab, x_scales)
+        load_scale_rows(nc.gpsimd, w2_s, w2_scales)
 
         nc.scalar.activation(gain[:], gn_t[:], COPY, scale=0.0625)
-        x_tab = sb("x_tab", [P, T], U32, "gn_then_x")
-        nc.sync.dma_start(x_tab[:].bitcast(I32), words_of(x_words))
 
-        ds_g = reuse.tile([P, H], U8, name="ds_g", align_bytes=64, offset=8 * N - H // 2)
+        ds_g = reuse2.tile([P, H], U8, name="ds_g", align_bytes=64, offset=S // 2)
         nc.vector.tensor_copy(ds_g[:], ds_tab[:].indirect(k1_l[:]))
         key_s = sb("key_s", [P, H], U8)
         nc.vector.tensor_copy(
@@ -80,22 +82,22 @@ def tile_picked_kmixirelay_none_p_kernel(
             ds_g[:].rearrange("p (mm i t) -> p mm t i", t=PACK, i=16),
         )
         for j in range(1, PACK):
-            nc.sync.dma_start(key_s[j:P:QUAD, :].bitcast(I32), key_s[8 * j : P : QUAD, :].bitcast(I32))
-        w_t = reuse.tile([P, 2 * N], U32, name="w_t", align_bytes=64, offset=0)
-        w1_s = reuse.tile([P, N], U8, name="w1_s", align_bytes=64, offset=8 * N)
+            nc.scalar.dma_start(key_s[j:P:QUAD, :].bitcast(I32), key_s[8 * j : P : QUAD, :].bitcast(I32))
+        w1_s = reuse2.tile([P, N], U8, name="w1_s", align_bytes=64, offset=2 * S)
+        load_scale_rows(nc.scalar, w1_s, w1_scales)
+
+        xq_s = reuse2.tile([P, S], U8, name="xq_s", align_bytes=64, offset=0)
+        nc.vector.tensor_copy(xq_s[:], xs_tab[:].indirect(offs_l[:]))
+        two_s = reuse2.tile([P, S], U8, name="two_s", align_bytes=64, offset=S)
+        nc.vector.tensor_copy(two_s[:], xs_tab[:].indirect(two_l[:]))
+
+        d_g = reuse.tile([P, H], U32, name="d_g", align_bytes=64, offset=0)
+        nc.vector.tensor_copy(d_g[:], d_tab[:].indirect(k1_l[:]))
+        w_t = sb("w_t", [P, 2 * N], U32, "d_tab_then_w")
         w2_t = w_t[:, 0:N]
         w1_t = w_t[:, N : 2 * N]
         nc.sync.dma_start(w2_t.bitcast(I32), words_of(w2_words))
         nc.sync.dma_start(w1_t.bitcast(I32), words_of(w1_words))
-        load_scale_rows([nc.sync] * PACK, w1_s, w1_scales)
-
-        xq_s = sb("xq_s", [P, S], U8)
-        nc.vector.tensor_copy(xq_s[:], xs_tab[:].indirect(offs_l[:]))
-
-        d_g = sb("d_g", [P, H], U32)
-        two_s = sb("two_s", [P, S], U8)
-        nc.vector.tensor_copy(d_g[:], d_tab[:].indirect(k1_l[:]))
-        nc.vector.tensor_copy(two_s[:], xs_tab[:].indirect(two_l[:]))
         key_w = sb("key_w", [P, H], U32)
         nc.vector.tensor_copy(
             key_w[:].rearrange("p (t mm i) -> p mm t i", t=PACK, i=4),
@@ -106,7 +108,7 @@ def tile_picked_kmixirelay_none_p_kernel(
         h_sb = [[sb("h_sb%d_%d" % (t, u), [P, HALF], F32) for u in range(2)] for t in range(TILES)]
         ds = [sb("ds%d" % t, [P, S], F32) for t in range(TILES)]
 
-        xq_w = sb("xq_w", [P, S], U32)
+        xq_w = reuse.tile([P, S], U32, name="xq_w", align_bytes=64, offset=0)
         s_bank = [psum.tile([P, PACK, HALF], F32, name="s_bank%d" % u) for u in range(2)]
 
         def score(u):
@@ -121,7 +123,7 @@ def tile_picked_kmixirelay_none_p_kernel(
 
         def project(u):
             cols = slice(u * HALF, (u + 1) * HALF)
-            two_w = sb("two_w%d" % u, [P, HALF], U32, "two_w")
+            two_w = reuse.tile([P, HALF], U32, name="two_w%d" % u, tag="two_w", align_bytes=64, offset=4 * S)
             nc.vector.tensor_copy(two_w[:], x_tab[:].indirect(two_l[:, u * HALF_COLS : (u + 1) * HALF_COLS]))
             for t in range(TILES):
                 mc = slice(t * P, (t + 1) * P)
@@ -169,7 +171,7 @@ def tile_picked_kmixirelay_none_p_kernel(
                 got = sb("got%d_%d" % (t, u), [P, HALF], F32)
                 nc.scalar.activation(got[:], ds[t][:].indirect(n2_l[:, u * HALF_COLS : (u + 1) * HALF_COLS]), COPY)
                 nc.vector.tensor_tensor(res[:, cols], h_sb[t][u][:], got[:], MAX)
-            nc.sync.dma_start(out[t * P : (t + 1) * P, :], res[:])
+                nc.sync.dma_start(out[t * P : (t + 1) * P, cols], res[:, cols])
 
         scatter_second(0)
         for t in range(TILES):

@@ -23,6 +23,8 @@ GROUP = 16
 HALF = S // 2
 HALF_COLS = HALF // GROUP
 TILES = N // P
+EARLY = 2
+WINDOW = 384
 
 
 def tile_picked_kmixirelay_none_p_kernel(
@@ -105,15 +107,22 @@ def tile_picked_kmixirelay_none_p_kernel(
         )
 
         h_bank = [psum.tile([P, S], F32, name="h_bank%d" % t) for t in range(TILES)]
-        h_sb = [[sb("h_sb%d_%d" % (t, u), [P, HALF], F32) for u in range(2)] for t in range(TILES)]
-        ds = [sb("ds%d" % t, [P, S], F32) for t in range(TILES)]
-
+        h_sb = [sb("h_sb%d" % t, [P, S], F32) for t in range(TILES)]
+        ds = [sb("ds%d" % t, [P, WINDOW], F32) for t in range(TILES)]
         xq_w = reuse.tile([P, S], U32, name="xq_w", align_bytes=64, offset=0)
+        two_w = reuse.tile([P, S], U32, name="two_w", align_bytes=64, offset=4 * S)
         s_bank = [psum.tile([P, PACK, HALF], F32, name="s_bank%d" % u) for u in range(2)]
+        z_w = sb("z_w", [P, S], U32)
+        z_s = sb("z_s", [P, S], U8)
+        first, second, whole = slice(0, HALF), slice(HALF, S), slice(0, S)
 
-        def score(u):
-            cols = slice(u * HALF, (u + 1) * HALF)
-            nc.vector.tensor_copy(xq_w[:, cols], x_tab[:].indirect(offs_l[:, u * HALF_COLS : (u + 1) * HALF_COLS]))
+        def entries(lst, cols):
+            return lst[:, cols.start // GROUP : cols.stop // GROUP]
+
+        def pick(dst, lst, cols):
+            nc.vector.tensor_copy(dst[:, cols], x_tab[:].indirect(entries(lst, cols)))
+
+        def score(u, cols):
             for t in range(PACK):
                 kc = slice(t * P, (t + 1) * P)
                 nc.tensor.matmul_mx(
@@ -121,60 +130,67 @@ def tile_picked_kmixirelay_none_p_kernel(
                     rhs=xq_w[:, cols].bitcast(FP8X4), rhs_scale=xq_s[:, cols], start=True, stop=True,
                 )
 
-        def project(u):
-            cols = slice(u * HALF, (u + 1) * HALF)
-            two_w = reuse.tile([P, HALF], U32, name="two_w%d" % u, tag="two_w", align_bytes=64, offset=4 * S)
-            nc.vector.tensor_copy(two_w[:], x_tab[:].indirect(two_l[:, u * HALF_COLS : (u + 1) * HALF_COLS]))
-            for t in range(TILES):
-                mc = slice(t * P, (t + 1) * P)
-                nc.tensor.matmul_mx(
-                    out=h_bank[t][:, cols], lhsT=w2_t[:, mc].bitcast(FP8X4), lhsT_scale=w2_s[:, mc],
-                    rhs=two_w[:].bitcast(FP8X4), rhs_scale=two_s[:, cols], start=True, stop=False,
-                )
+        def w2_pass(t, cols, start):
+            mc = slice(t * P, (t + 1) * P)
+            nc.tensor.matmul_mx(
+                out=h_bank[t][:, cols], lhsT=w2_t[:, mc].bitcast(FP8X4), lhsT_scale=w2_s[:, mc],
+                rhs=two_w[:, cols].bitcast(FP8X4), rhs_scale=two_s[:, cols], start=start, stop=not start,
+            )
 
-        score(0)
-        project(0)
-        score(1)
-        for u in range(2):
-            cols = slice(u * HALF, (u + 1) * HALF)
-            lcols = slice(u * HALF_COLS, (u + 1) * HALF_COLS)
+        def w1_pass(t, cols, start):
+            mc = slice(t * P, (t + 1) * P)
+            nc.tensor.matmul_mx(
+                out=h_bank[t][:, cols], lhsT=w1_t[:, mc].bitcast(FP8X4), lhsT_scale=w1_s[:, mc],
+                rhs=z_w[:, cols].bitcast(FP8X4), rhs_scale=z_s[:, cols], start=start, stop=not start,
+            )
+
+        def quantise(u, cols):
             z_bf = sb("z_bf%d" % u, [P, HALF, PACK], BF16, "z_bf")
             nc.vector.tensor_tensor(
                 z_bf[:], s_bank[u][:].rearrange("p t n -> p n t"), gain[:].unsqueeze(1).broadcast_to([P, HALF, PACK]), MULT
             )
-            if u == 1:
-                project(1)
-            z_w = sb("z_w%d" % u, [P, HALF], U32)
-            z_s = sb("z_s%d" % u, [P, HALF], U8)
-            nc.vector.quantize_mx(out=z_w[:].bitcast(FP8X4), scales=z_s[:], in_=z_bf[:].rearrange("p n t -> p (n t)"))
-            for t in range(TILES):
-                mc = slice(t * P, (t + 1) * P)
-                nc.tensor.matmul_mx(
-                    out=h_bank[t][:, cols], lhsT=w1_t[:, mc].bitcast(FP8X4), lhsT_scale=w1_s[:, mc],
-                    rhs=z_w[:].bitcast(FP8X4), rhs_scale=z_s[:], start=False, stop=True,
-                )
-                if u == 0 and t == 0:
-                    nc.scalar.copy(h_sb[t][u][:], h_bank[t][:, cols])
-                else:
-                    nc.vector.tensor_copy(h_sb[t][u][:], h_bank[t][:, cols])
-            if u == 0:
-                for t in range(TILES):
-                    nc.scalar.activation(ds[t][:].indirect(n1_l[:, lcols]), h_sb[t][u][:], COPY)
+            nc.vector.quantize_mx(out=z_w[:, cols].bitcast(FP8X4), scales=z_s[:, cols], in_=z_bf[:].rearrange("p n t -> p (n t)"))
 
-        def scatter_second(t):
-            nc.scalar.activation(ds[t][:].indirect(n1_l[:, HALF_COLS:]), h_sb[t][1][:], COPY)
+        def scatter(t, cols):
+            nc.scalar.activation(ds[t][:].indirect(entries(n1_l, cols)), h_sb[t][:, cols], COPY)
 
-        def fetch(t):
-            res = sb("res%d" % t, [P, S], F32)
-            for u in range(2):
-                cols = slice(u * HALF, (u + 1) * HALF)
-                got = sb("got%d_%d" % (t, u), [P, HALF], F32)
-                nc.scalar.activation(got[:], ds[t][:].indirect(n2_l[:, u * HALF_COLS : (u + 1) * HALF_COLS]), COPY)
-                nc.vector.tensor_tensor(res[:, cols], h_sb[t][u][:], got[:], MAX)
-                nc.sync.dma_start(out[t * P : (t + 1) * P, cols], res[:, cols])
+        def fetch(t, cols):
+            got = sb("got%d_%d" % (t, cols.start), [P, cols.stop - cols.start], F32)
+            res = sb("res%d_%d" % (t, cols.start), [P, cols.stop - cols.start], F32)
+            nc.scalar.activation(got[:], ds[t][:].indirect(entries(n2_l, cols)), COPY)
+            nc.vector.tensor_tensor(res[:], h_sb[t][:, cols], got[:], MAX)
+            nc.sync.dma_start(out[t * P : (t + 1) * P, cols], res[:])
 
-        scatter_second(0)
-        for t in range(TILES):
-            if t + 1 < TILES:
-                scatter_second(t + 1)
-            fetch(t)
+        pick(xq_w, offs_l, first)
+        score(0, first)
+        pick(two_w, two_l, first)
+        for t in range(EARLY):
+            w2_pass(t, first, True)
+        pick(xq_w, offs_l, second)
+        score(1, second)
+        pick(two_w, two_l, second)
+
+        quantise(0, first)
+        for t in range(EARLY):
+            w1_pass(t, first, False)
+            if t == 0:
+                nc.scalar.copy(h_sb[t][:, first], h_bank[t][:, first])
+            else:
+                nc.vector.tensor_copy(h_sb[t][:, first], h_bank[t][:, first])
+            scatter(t, first)
+
+        quantise(1, second)
+        for t in range(EARLY):
+            w2_pass(t, second, True)
+            w1_pass(t, second, False)
+            nc.vector.tensor_copy(h_sb[t][:, second], h_bank[t][:, second])
+            scatter(t, second)
+        for t in range(EARLY, TILES):
+            w1_pass(t, whole, True)
+            w2_pass(t, whole, False)
+            nc.vector.tensor_copy(h_sb[t][:], h_bank[t][:])
+            scatter(t, whole)
+        for t in range(TILES - 1):
+            fetch(t, whole)
+        fetch(TILES - 1, first)
+        fetch(TILES - 1, second)

from contextlib import ExitStack

import concourse.mybir as mybir

K, T, S, N, G, H = 512, 2048, 256, 512, 2048, 512
FLOPS = 2 * S * (K * H + H * N + K * N)

F32 = mybir.dt.float32
BF16 = mybir.dt.bfloat16
I32 = mybir.dt.int32
U32 = mybir.dt.uint32
U16 = mybir.dt.uint16
U8 = mybir.dt.uint8
FP8X4 = mybir.dt.float8_e4m3fn_x4
COPY = mybir.ActivationFunctionType.Copy
MULT = mybir.AluOpType.mult
MAX = mybir.AluOpType.max

P = 128
PACK = 4
QUAD = 32
GROUP = 16
HALF = S // 2
HALF_COLS = HALF // GROUP
TILES = N // P
EARLY = 2
WINDOW = 384


def tile_picked_kmixirelay_none_p_kernel(
    tc, x_words, x_scales, d_words, d_scales, gn, w1_words, w1_scales, w2_words, w2_scales, offs, k1, two, n1, n2, out
):
    nc = tc.nc

    def words_of(dram):
        return dram[0].rearrange("p n t -> p (n t)").bitcast(I32)

    with ExitStack() as ctx:
        keep = ctx.enter_context(tc.tile_pool(name="keep", bufs=1))
        reuse = ctx.enter_context(tc.tile_pool(name="reuse", bufs=1))
        reuse2 = ctx.enter_context(tc.tile_pool(name="reuse2", bufs=1))
        psum = ctx.enter_context(tc.psum_pool(name="psum", bufs=1))

        def sb(name, shape, dtype, tag=None):
            return keep.tile(shape, dtype, name=name, tag=tag or name, align_bytes=64)

        k1_l = sb("k1_l", [P, H // GROUP], U16)
        offs_l = sb("offs_l", [P, S // GROUP], U16)
        two_l = sb("two_l", [P, S // GROUP], U16)
        n1_l = sb("n1_l", [P, S // GROUP], U16)
        n2_l = sb("n2_l", [P, S // GROUP], U16)
        d_tab = sb("d_tab", [P, G], U32, "d_tab_then_w")
        x_tab = sb("x_tab", [P, T], U32)
        ds_tab = sb("ds_tab", [P, G], U8)
        xs_tab = reuse.tile([P, T], U8, name="xs_tab", align_bytes=64, offset=0)
        w2_s = sb("w2_s", [P, N], U8)
        gn_t = sb("gn_t", [P, PACK], F32)
        gain = sb("gain", [P, PACK], F32)

        def load_scale_rows(queue, tile, dram):
            rows = dram[0].bitcast(I32)
            for j in range(PACK):
                queue.dma_start(tile[j:P:QUAD, :].bitcast(I32), rows[j:16:PACK, :])

        nc.vector.memset(ds_tab[:, 0 : G // 2].bitcast(I32), 0)
        nc.gpsimd.memset(ds_tab[:, G // 2 : G].bitcast(I32), 0)
        nc.vector.memset(xs_tab[:].bitcast(I32), 0)
        nc.scalar.dma_start(gn_t[:], gn.rearrange("(p t) o -> p (t o)", t=PACK))
        for tile, dram in ((k1_l, k1), (offs_l, offs), (two_l, two), (n1_l, n1), (n2_l, n2)):
            nc.sync.dma_start(tile[:], dram)
        nc.scalar.dma_start(ds_tab[0:P:8, :].bitcast(I32), d_scales[0].bitcast(I32))
        nc.sync.dma_start(d_tab[:].bitcast(I32), words_of(d_words))
        nc.sync.dma_start(x_tab[:].bitcast(I32), words_of(x_words))
        load_scale_rows(nc.scalar, xs_tab, x_scales)
        load_scale_rows(nc.gpsimd, w2_s, w2_scales)

        nc.scalar.activation(gain[:], gn_t[:], COPY, scale=0.0625)

        ds_g = reuse2.tile([P, H], U8, name="ds_g", align_bytes=64, offset=S // 2)
        nc.vector.tensor_copy(ds_g[:], ds_tab[:].indirect(k1_l[:]))
        key_s = sb("key_s", [P, H], U8)
        nc.vector.tensor_copy(
            key_s[:].rearrange("p (t mm i) -> p mm t i", t=PACK, i=16),
            ds_g[:].rearrange("p (mm i t) -> p mm t i", t=PACK, i=16),
        )
        for j in range(1, PACK):
            nc.scalar.dma_start(key_s[j:P:QUAD, :].bitcast(I32), key_s[8 * j : P : QUAD, :].bitcast(I32))
        w1_s = reuse2.tile([P, N], U8, name="w1_s", align_bytes=64, offset=2 * S)
        load_scale_rows(nc.scalar, w1_s, w1_scales)

        xq_s = reuse2.tile([P, S], U8, name="xq_s", align_bytes=64, offset=0)
        nc.vector.tensor_copy(xq_s[:], xs_tab[:].indirect(offs_l[:]))
        two_s = reuse2.tile([P, S], U8, name="two_s", align_bytes=64, offset=S)
        nc.vector.tensor_copy(two_s[:], xs_tab[:].indirect(two_l[:]))

        d_g = reuse.tile([P, H], U32, name="d_g", align_bytes=64, offset=0)
        nc.vector.tensor_copy(d_g[:], d_tab[:].indirect(k1_l[:]))
        w_t = sb("w_t", [P, 2 * N], U32, "d_tab_then_w")
        w2_t = w_t[:, 0:N]
        w1_t = w_t[:, N : 2 * N]
        nc.sync.dma_start(w2_t.bitcast(I32), words_of(w2_words))
        nc.sync.dma_start(w1_t.bitcast(I32), words_of(w1_words))
        key_w = sb("key_w", [P, H], U32)
        nc.vector.tensor_copy(
            key_w[:].rearrange("p (t mm i) -> p mm t i", t=PACK, i=4),
            d_g[:].rearrange("p (mm i t) -> p mm t i", t=PACK, i=4),
        )

        h_bank = [psum.tile([P, S], F32, name="h_bank%d" % t) for t in range(TILES)]
        h_sb = [sb("h_sb%d" % t, [P, S], F32) for t in range(TILES)]
        ds = [sb("ds%d" % t, [P, WINDOW], F32) for t in range(TILES)]
        xq_w = reuse.tile([P, S], U32, name="xq_w", align_bytes=64, offset=0)
        two_w = reuse.tile([P, S], U32, name="two_w", align_bytes=64, offset=4 * S)
        s_bank = [psum.tile([P, PACK, HALF], F32, name="s_bank%d" % u) for u in range(2)]
        z_w = sb("z_w", [P, S], U32)
        z_s = sb("z_s", [P, S], U8)
        first, second, whole = slice(0, HALF), slice(HALF, S), slice(0, S)

        def entries(lst, cols):
            return lst[:, cols.start // GROUP : cols.stop // GROUP]

        def pick(dst, lst, cols):
            nc.vector.tensor_copy(dst[:, cols], x_tab[:].indirect(entries(lst, cols)))

        def score(u, cols):
            for t in range(PACK):
                kc = slice(t * P, (t + 1) * P)
                nc.tensor.matmul_mx(
                    out=s_bank[u][:, t, :], lhsT=key_w[:, kc].bitcast(FP8X4), lhsT_scale=key_s[:, kc],
                    rhs=xq_w[:, cols].bitcast(FP8X4), rhs_scale=xq_s[:, cols], start=True, stop=True,
                )

        def w2_pass(t, cols, start):
            mc = slice(t * P, (t + 1) * P)
            nc.tensor.matmul_mx(
                out=h_bank[t][:, cols], lhsT=w2_t[:, mc].bitcast(FP8X4), lhsT_scale=w2_s[:, mc],
                rhs=two_w[:, cols].bitcast(FP8X4), rhs_scale=two_s[:, cols], start=start, stop=not start,
            )

        def w1_pass(t, cols, start):
            mc = slice(t * P, (t + 1) * P)
            nc.tensor.matmul_mx(
                out=h_bank[t][:, cols], lhsT=w1_t[:, mc].bitcast(FP8X4), lhsT_scale=w1_s[:, mc],
                rhs=z_w[:, cols].bitcast(FP8X4), rhs_scale=z_s[:, cols], start=start, stop=not start,
            )

        def quantise(u, cols):
            z_bf = sb("z_bf%d" % u, [P, HALF, PACK], BF16, "z_bf")
            nc.vector.tensor_tensor(
                z_bf[:], s_bank[u][:].rearrange("p t n -> p n t"), gain[:].unsqueeze(1).broadcast_to([P, HALF, PACK]), MULT
            )
            nc.vector.quantize_mx(out=z_w[:, cols].bitcast(FP8X4), scales=z_s[:, cols], in_=z_bf[:].rearrange("p n t -> p (n t)"))

        def scatter(t, cols):
            nc.scalar.activation(ds[t][:].indirect(entries(n1_l, cols)), h_sb[t][:, cols], COPY)

        def fetch(t, cols):
            got = sb("got%d_%d" % (t, cols.start), [P, cols.stop - cols.start], F32)
            res = sb("res%d_%d" % (t, cols.start), [P, cols.stop - cols.start], F32)
            nc.scalar.activation(got[:], ds[t][:].indirect(entries(n2_l, cols)), COPY)
            nc.vector.tensor_tensor(res[:], h_sb[t][:, cols], got[:], MAX)
            nc.sync.dma_start(out[t * P : (t + 1) * P, cols], res[:])

        pick(xq_w, offs_l, first)
        score(0, first)
        pick(two_w, two_l, first)
        for t in range(EARLY):
            w2_pass(t, first, True)
        pick(xq_w, offs_l, second)
        score(1, second)
        pick(two_w, two_l, second)

        quantise(0, first)
        for t in range(EARLY):
            w1_pass(t, first, False)
            if t == 0:
                nc.scalar.copy(h_sb[t][:, first], h_bank[t][:, first])
            else:
                nc.vector.tensor_copy(h_sb[t][:, first], h_bank[t][:, first])
            scatter(t, first)

        quantise(1, second)
        for t in range(EARLY):
            w2_pass(t, second, True)
            w1_pass(t, second, False)
            nc.vector.tensor_copy(h_sb[t][:, second], h_bank[t][:, second])
            scatter(t, second)
        for t in range(EARLY, TILES):
            w1_pass(t, whole, True)
            w2_pass(t, whole, False)
            nc.vector.tensor_copy(h_sb[t][:], h_bank[t][:])
            scatter(t, whole)
        for t in range(TILES - 1):
            fetch(t, whole)
        fetch(TILES - 1, first)
        fetch(TILES - 1, second)
